import numpy as np, ml_dtypes
CORES = [36,164,52,180,100,228,116,244]
N = 8
import mx_ref
BF = ml_dtypes.bfloat16
def gentries(a):
    return np.ascontiguousarray(a.reshape(8, 16, -1).transpose(0, 2, 1)).reshape(8, -1)
def gtable(e):
    e = np.asarray(e); return np.ascontiguousarray(e.reshape(8, -1, 16).transpose(0, 2, 1)).reshape(128, -1).astype(np.int32)
def gcols(t, e):
    v = np.concatenate([t.reshape(8, 16, -1, 4), np.zeros((8, 16, 1, 4), BF)], axis=2)
    return np.ascontiguousarray(np.stack([v[g][:, e[g]] for g in range(8)])).reshape(128, -1)
def tile(rs):
    return np.stack(rs, axis=2).reshape(128, -1).astype(BF)
def pick(q, e):
    c = np.concatenate([q[0].reshape(128, -1, 4), np.zeros((128, 1, 4), np.uint8)], axis=1); s = np.concatenate([q[1], np.ones((16, 1), np.uint8)], axis=1)
    return (np.ascontiguousarray(c[:, e].reshape(128, -1)), np.ascontiguousarray(s[:, e]))
def join(*qs):
    return (np.concatenate([q[0] for q in qs], axis=1), np.concatenate([q[1] for q in qs], axis=1))
def put(q, e, v):
    c, s = q[0].reshape(128, -1, 4).copy(), q[1].copy(); c[:, e] = v[0].reshape(128, -1, 4); s[:, e] = v[1]
    return (c.reshape(128, -1), s)
def pk(c, s):
    return (np.ascontiguousarray(c), mx_ref.live(s))
def emit(q):
    return q[0], q[1]
def packed(v, rng):
    q = [mx_ref.quantize(np.ascontiguousarray(v[r])) for r in range(N)]
    return np.stack([a for a, b in q]), np.stack([mx_ref.plane(b, rng) for a, b in q])
def values_of_codes():
    e, c = np.zeros((128, 128, 4), np.float32), np.zeros((128, 2, 4), np.uint8)
    e[np.arange(128), np.arange(128), 0] = 1
    c[:127, :, 0] = np.arange(256).reshape(2, 128).T[:127]
    return mx_ref.matmul(mx_ref.quantize(e.reshape(128, 512).astype(BF)), (c.reshape(128, 8), np.full((16, 2), 127, np.uint8))).T.reshape(-1).astype(np.float64)
CODE_VALUE, SCALE_VALUE = values_of_codes(), 2.0 ** (np.arange(256) - 127.0)
def decode(q):
    return (CODE_VALUE[q[0]].reshape(16, 8, -1, 4) * SCALE_VALUE[q[1]][:, None, :, None] + 0.0).reshape(128, -1).astype(np.float32)
def f(rng, *shape):
    return mx_ref.flush((rng.standard_normal(shape, dtype=np.float32) * np.exp2(rng.integers(-2, 3, shape[:-1] + (1,)))).astype(BF))
def wide(rng, *shape, cols=0):
    v = rng.standard_normal(shape, dtype=np.float32) * np.exp2(rng.integers(-12, 13, shape)).astype(np.float32)
    if cols: v *= np.repeat(np.exp2(rng.integers(-cols, cols + 1, shape[:-2] + (1, shape[-1] // 4))) * (rng.random(shape[:-2] + (1, shape[-1] // 4)) > 0.0625), 4, axis=-1).astype(np.float32)
    return mx_ref.flush(v.astype(BF))
C, F = 352, 176
STEP = [2, 4, 1]
def big(v):
    v = v.astype(np.float32)
    v[np.abs(v) < np.float32(2.0 ** -16)] = 0
    return v.astype(BF)
def numbers_of(rng):
    return {"x": big(f(rng, N, 128, 4 * C)), "u": np.array(f(rng, N, 128, 512)), "v": np.array(f(rng, N, 128, 512))}
def stored(q):
    return {k: np.stack([gtable(q[i, r]) for r in range(N)]) for i, k in enumerate(("pl", "dl", "kl"))}
def lists(rng):
    return stored(rng.permuted(np.tile(np.arange(C), (3, N, 8, 1)), axis=3))
def layers(rng):
    return big(f(rng, N, 128, 2048)).reshape(N, 8, 16, 4, 8, 16, 4)
def weights(rng, w):
    c, s = packed(np.ascontiguousarray(w).reshape(N, 128, 2048), rng)
    return {"wc": c, "ws": s}
def deciding(d):
    u = d["u"].reshape(N, 8, 16, 8, 16, 4)
    u[:, :, :, :, :4] = 0
    return u
def setup_inputs(rng):
    return {**numbers_of(rng), **lists(rng), **weights(rng, layers(rng))}
def setup_inputs_ties(rng):
    d = numbers_of(rng)
    o = rng.permutation(N)
    k = rng.integers(-1, 2, (N, 8, C, 4)).astype(np.float32)
    k[o[1]] = 1
    a = np.exp2(rng.integers(-3, 4, 8).astype(np.float32))
    x = d["x"].reshape(N, 8, 16, C, 4)
    x[:, :, 0] = k.astype(BF)
    x[:, :, 4:6] = 0
    x[:, :, 4, :, 0] = 1.96875 * 2.0 ** 5
    x[:, :, 5, :, 0] = 1.125 * 2.0 ** -8
    x[:, :, 8:] = 0
    x[:, :, 8, :, 0] = (-1.125 * a)[None, :, None].astype(BF)
    x[:, :, 10, :, 0] = (-0.0703125 * a)[None, :, None].astype(BF)
    c = np.ones(N, np.float32)
    c[o[0]] = 0
    c[o[2]] = -1
    u = deciding(d)
    w = layers(rng)
    w[:] = 0
    for g in range(8):
        w[:, g, 8, 0, g, 8, 0] = -28.0
        w[:, g, 5, 0, g, 11, 0] = 4.0
        for b in range(4):
            w[:, g, 10, b, g, 9, 0] = -2.0 ** (b - 5)
            u[:, g, 0, g, b, b] = c.astype(BF)
    return {**d, **lists(rng), **weights(rng, w)}
def setup_inputs_near(rng):
    d = numbers_of(rng)
    o = rng.permutation(N) % 4
    x = d["x"].astype(np.float32).reshape(N, 8, 16, C, 4)
    x[:, :, :10] = 0
    u = deciding(d)
    w = layers(rng)
    w[:, :, :10] = 0
    w[:, :, :, :, :, :10] = 0
    for r in range(N):
        k = 2.0 ** -30 if o[r] == 0 else 1.0
        s = rng.integers(-1, 2, (8, C, 4)).astype(np.float64)
        if o[r] == 3:
            x[r] = 0
            x[r, :, 2, :, 0] = 2.0 ** -30
            x[r, :, 7, :, 0] = 2.0 ** -30
            x[r, :, 8] = rng.choice([-1.0, 1.0], (8, C, 4)) * 2.0 ** -29
            x[r, :, 9, :, 0] = 2.0 ** -29
            w[r] = 0
            for g in range(8):
                w[r, g, 7, 0, g, 2, 0] = 32.0
                for b in range(4):
                    w[r, g, 8, b, g, 0, b] = 2.0 ** -10
                    w[r, g, 8, b, g, 1, b] = -2.0 ** -10
                    w[r, g, 0, b, g, 3, b] = 128.0
                    w[r, g, 8, b, g, 5, b] = 2.0 ** -11
                    w[r, g, 0, b, g, 5, b] = 0.5
                    u[r, g, 0, g, b, b] = 1.125 * 2.0 ** -30
                    u[r, g, 1, g, b, b] = 2.0 ** -30
            continue
        if o[r] == 1:
            s *= np.exp2(rng.integers(0, 3, (8, C, 1)).astype(np.float64))
            x[r, :, 0] = 1.125 * s
            x[r, :, 1] = -s
            x[r, :, 7, :, 0] = 1.96875 * 2.0 ** 13
        else:
            x[r, :, 0] = 1.125 * s * k
            x[r, :, 1] = -1.25 * s * k
            x[r, :, 2, :, 0] = k
        for g, j in zip(rng.permutation(8)[:4], [0, C - 1, int(rng.integers(C)), int(rng.integers(C))]): x[r, g, 0, j, 0] = 2.0 ** 30 * rng.choice([-1.0, 1.0])
        for g in range(8):
            for b in range(4):
                u[r, g, 0, g, b, b] = 1.0 if o[r] == 1 else 1.125 * k
                u[r, g, 1, g, b, b] = k
    d["x"] = x.reshape(N, 128, 4 * C).astype(BF)
    return {**d, **lists(rng), **weights(rng, w)}
def setup_inputs_late(rng):
    d = numbers_of(rng)
    o = rng.permutation(N) % 4
    e = np.stack([o & 1, o >> 1, (o + 1) & 1, ((o + 1) >> 1) & 1], axis=1) * 2.0 - 1.0
    d["x"].reshape(N, 8, 16, C, 4)[:, :, 0] = e[:, None, None, :].astype(np.float32).astype(BF)
    u = deciding(d)
    for g in range(8):
        for b in range(4): u[:, g, 0, g, b, b] = 1
    w = layers(rng)
    w[:, :, :, :, :, 0] = (w[:, :, :, :, :, 0].astype(np.float32) * 4).astype(BF)
    return {**d, **lists(rng), **weights(rng, w)}
def setup_inputs_ends(rng):
    d = numbers_of(rng)
    o, e = rng.permutation(N) % 4, rng.permutation(N) % 4
    s = rng.choice([-1.0, 1.0], (N, 128, C, 4))
    s[o == 0] = -1
    s[o == 1] = rng.choice([-1.0, 1.0], (N, 1, C, 1))[o == 1]
    x = s * (0.76 + 0.02 * rng.random((N, 128, C, 4))) * 2.0 ** 30
    x[o == 3] = 2.0 ** -30
    size = np.where(o == 3, 2.0 ** -30, 2.0 ** 30)
    k = np.stack([rng.permutation(8) for r in range(N)])
    a = np.stack([k & 1, (k >> 1) & 1, k >> 2, (k ^ (k >> 1)) & 1], axis=2) * 2.0 - 1.0
    a[k < 2] = 0
    a = a * size[:, None, None]
    deciding(d)[:, :, :, :, :4] = a.astype(np.float32).astype(BF)[:, None, None, :, :, None]
    v = rng.choice([-1.0, 1.0], (N, 128, 512)) * size[:, None, None]
    q = rng.integers(0, C, (3, N, 8, C))
    q[:, e == 0] = C - 1
    q[:, e == 1] = 0
    q[:, e == 1, 7] = C - 1
    q[:, e == 2] = rng.integers(0, 2, (3, 1, 8, C)) * (C - 1)
    w = np.zeros((N, 128, 4, 128, 4), np.float32)
    i = np.arange(128)
    for b in range(4): w[:, i, b, i, b] = np.where(o[:, None] == 3, 128.0, np.where((i >> 4) % 2 == 0, -0.25, 2.0 ** -12)[None, :])
    d["x"] = x.astype(np.float32).reshape(N, 128, 4 * C).astype(BF)
    d["v"] = v.astype(np.float32).astype(BF)
    return {**d, **stored(q), **weights(rng, w.astype(BF))}
def setup_inputs_spread(rng):
    d = setup_inputs(rng)
    d["x"] = big(wide(rng, N, 128, 4 * C, cols=6))
    return d
def check_inputs(d):
    b = []
    for k in ("x", "u", "v"):
        a = np.abs(d[k].astype(np.float32))
        if not (np.isfinite(a).all() and ((a == 0) | (a >= 2.0 ** -30) & (a <= 2.0 ** 30)).all()): b.append("a value of " + k)
    for k in ("pl", "dl", "kl"):
        if not ((d[k] >= 0) & (d[k] < C)).all(): b.append("an entry of " + k)
    none, least, most = [emit(mx_ref.quantize(np.full((128, 16), k, np.float32).astype(BF)))[1][0, 0] for k in (0.0, 2.0 ** -12, 2.0 ** 7)]
    for r in range(N):
        if ((d["wc"][r] == 0x7F) | (d["wc"][r] == 0xFF)).any(): b.append("wc: a code that is no number")
        s = mx_ref.live(d["ws"][r])
        if ((s != none) & ((s < least) | (s > most))).any(): b.append("ws: a scale out of range")
        if (((d["wc"][r].reshape(16, 8, 512, 4) & 0x7F) != 0) & (s == none)[:, None, :, None]).any(): b.append("wc: a code other than zero under the scale of zeros")
    return b
def at(a, e):
    return np.take_along_axis(a, e, axis=1)
def reference(x, u, v, pl, dl, kl, wc, ws):
    qu = [mx_ref.quantize(u[r]) for r in range(N)]
    lay = [pk(wc[r], ws[r]) for r in range(N)]
    drawn = [np.stack([gentries(pl[r]), gentries(dl[r]), gentries(kl[r])]).astype(np.int64) for r in range(N)]
    link = [drawn[r] for r in range(N)]
    now = [x[r] for r in range(N)]
    for step in STEP:
        made = []
        for r in range(N):
            bit = mx_ref.matmul(qu[r], mx_ref.quantize(now[r])).reshape(8, 16, C) > 0
            for j in range(2):
                p, d, k = link[r]
                one, two = at(bit[:, 2 * j], p), at(bit[:, 2 * j + 1], p)
                t = np.where(two, at(p, p), at(d, p))
                there = np.stack([at(p, t), at(d, t), at(k, t)])
                link[r] = np.where(one, there, np.where(two, drawn[r], np.stack([d, k, p])))
            p, d, k = link[r]
            z = ((gcols(now[r], p).astype(np.float32) + gcols(now[r], k).astype(np.float32)) * np.float32(0.5)).astype(BF)
            q = mx_ref.quantize(z)
            made.append(tile([mx_ref.matmul(pick(lay[r], np.arange(128 * b, 128 * b + 128)), q) * np.float32(0.03125) for b in range(4)]))
        new = []
        for r in range(N):
            i = (r - step) % N
            m = at(link[i][2], link[r][0])
            far = gcols(decode(mx_ref.quantize(made[i])).astype(BF), m[:, :F])
            own = gcols(made[r], m[:, F:])
            new.append((now[r].astype(np.float32) + np.concatenate([far, own], axis=1).astype(np.float32)).astype(BF))
        now = new
    y, lk = np.zeros((N, 128, C), np.float32), np.zeros((N, 8, 3 * C), np.float32)
    oc, osc = np.zeros((N, 128, 4 * C), np.uint8), np.zeros((N, 16, C), np.uint8)
    for r in range(N):
        q = mx_ref.quantize(now[r])
        y[r] = mx_ref.matmul(mx_ref.quantize(v[r]), q)
        lk[r] = np.concatenate([link[r][0], link[r][1], link[r][2]], axis=1)
        oc[r], osc[r] = emit(q)
    return {"y": y, "lk": lk, "oc": oc, "osc": osc}

@@ -1,0 +1,486 @@
+from concourse.bass import DstId, RemoteDMATransfer
+from concourse.mybir import dt, AluOpType as AO, ActivationFunctionType as AF
+
+C, F = 352, 176
+STEP = [2, 4, 1]
+MID = 176
+ROT, DRAWN = 368, 720
+B16, F32, I32, U16, U8, MXC = "bfloat16", "float32", "int32", "uint16", "uint8", "float8_e4m3fn_x4"
+
+SCRATCH = {
+    "tbi": ("sbuf", [128, 96], I32), "tbs": ("sbuf", [128, 256], B16), "ttb": ("sbuf", [128, 128], B16), "tf": ("sbuf", [128, 368], B16),
+    "ones": ("sbuf", [128, 512], B16), "eb": ("sbuf", [128, 2048], B16), "qe": ("sbuf", [128, 512], MXC), "se": ("sbuf", [128, 512], U8),
+    "ci": ("sbuf", [128, 16], I32), "cf": ("sbuf", [128, 64], F32), "rc": ("sbuf", [128, 40], F32), "lc": ("sbuf", [128, 32], F32),
+    "i2": ("sbuf", [128, 24], F32), "gam": ("sbuf", [128, 48], F32), "offi": ("sbuf", [128, 24], U16), "pk": ("sbuf", [128, 8], U16),
+    "wq": ("sbuf", [128, 512], MXC), "wp": ("sbuf", [128, 512], U8),
+    "ut": ("sbuf", [128, 512], B16), "qu": ("sbuf", [128, 128], MXC), "su": ("sbuf", [128, 128], U8),
+    "vt": ("sbuf", [128, 512], B16), "qv": ("sbuf", [128, 128], MXC), "sv": ("sbuf", [128, 128], U8),
+    "x0": ("sbuf", [128, 4 * C], B16), "x1": ("sbuf", [128, 4 * C], B16), "x2": ("sbuf", [128, 4 * C], B16), "x3": ("sbuf", [128, 4 * C], B16),
+    "xp": ("sbuf", [128, 4 * C], B16), "hp": ("sbuf", [128, 4 * C], B16), "zp": ("sbuf", [128, 4 * C], B16), "zt": ("sbuf", [128, 4 * C], B16),
+    "ft": ("sbuf", [128, 4 * F], B16),
+    "qx": ("sbuf", [128, C], MXC), "sx": ("sbuf", [128, C], U8), "qz": ("sbuf", [128, C], MXC), "sz": ("sbuf", [128, C], U8),
+    "bt": ("sbuf", [128, C], B16), "wa": ("sbuf", [128, 1088], B16), "wb": ("sbuf", [128, 1088], B16),
+    "gb": ("sbuf", [128, 384], B16), "gl": ("sbuf", [128, 384], B16), "mf": ("sbuf", [128, 384], B16), "mo": ("sbuf", [128, 384], B16),
+    "gt": ("sbuf", [128, 752], B16), "glt": ("sbuf", [128, 752], B16), "n1": ("sbuf", [128, 752], B16), "n2": ("sbuf", [128, 752], B16),
+    "kr": ("sbuf", [128, C], B16), "sm": ("sbuf", [128, 480], F32),
+    "o1": ("sbuf", [128, 32], U16), "o2": ("sbuf", [128, 32], U16), "op1": ("sbuf", [128, 32], U16), "ok": ("sbuf", [128, 32], U16),
+    "opi": ("sbuf", [128, 32], U16), "om": ("sbuf", [128, 16], U16), "oo": ("sbuf", [128, 16], U16),
+    "lkt": ("sbuf", [128, C], F32), "yt": ("sbuf", [128, C], F32),
+    "ps": ("psum", [128, 4096], F32),
+}
+for _r in range(3):
+    SCRATCH["opn%d" % _r] = ("sbuf", [128, 32], U16)
+    SCRATCH["ks%d" % _r] = ("sbuf", [128, 22], B16)
+    SCRATCH["pin%d" % _r] = ("sbuf", [128, 22], U16)
+    SCRATCH["kin%d" % _r] = ("sbuf", [128, 22], B16)
+    SCRATCH["qf%d" % _r] = ("sbuf", [128, F], MXC)
+    SCRATCH["sf%d" % _r] = ("sbuf", [128, F], U8)
+    SCRATCH["qin%d" % _r] = ("sbuf", [128, F], MXC)
+    SCRATCH["sin%d" % _r] = ("sbuf", [128, F], U8)
+SEMAPHORES = ["cv", "cs", "ct", "cg", "sent", "sty", "sta",
+              "ldp", "ldd", "ldk", "ldx0", "ldx1", "ldu", "ldv", "ldwc", "ldws"]
+SEMAPHORES += [k + str(r) for r in range(3) for k in ("ap", "ak", "ac", "as")]
+
+
+def make_tracker(g, T):
+    queues = {"v": g.vector, "s": g.scalar, "t": g.tensor, "g": g, "y": g.sync}
+    own = {"v": "cv", "s": "cs", "t": "ct", "g": "cg"}
+    count = {}
+    known = {q: {} for q in queues}
+    snaps = {}
+    hist = {}
+
+    def span(r):
+        n, lo, hi, st = r
+        return (n, lo // 512 * 512, (hi + 511) // 512 * 512, 1) if n == "ps" else r
+
+    def meet(a, b):
+        if a[1] >= b[2] or b[1] >= a[2]:
+            return False
+        return not (a[3] == b[3] and a[3] > 1 and (a[1] - b[1]) % a[3])
+
+    def note(r, write, tok):
+        r = span(r)
+        h = hist.setdefault(r[0], [])
+        if write and r[3] == 1:
+            h[:] = [e for e in h if not (r[1] <= e[0][1] and e[0][2] <= r[2])]
+        h.append((r, write, tok))
+
+    def wait(q, need):
+        for sem in sorted(need):
+            val = need[sem]
+            if known[q].get(sem, 0) >= val:
+                continue
+            if any(o != sem and known[q].get(o, 0) < need[o] and snaps.get((o, need[o]), {}).get(sem, 0) >= val for o in need):
+                continue
+            queues[q].wait_ge(T.sem[sem], val)
+        for sem in need:
+            known[q][sem] = max(known[q].get(sem, 0), need[sem])
+            for s, v in snaps.get((sem, need[sem]), {}).items():
+                known[q][s] = max(known[q].get(s, 0), v)
+
+    def deps(reads, writes):
+        need = {}
+        for rs, w in ((reads, False), (writes, True)):
+            for r in rs:
+                r = span(r)
+                for e, ew, tok in hist.get(r[0], []):
+                    if (w or ew) and meet(r, e):
+                        need[tok[0]] = max(need.get(tok[0], 0), tok[1])
+        return need
+
+    def emit(q, call, reads, writes, sem=None, inc=1):
+        wait(q, deps(reads, writes))
+        name = sem or own[q]
+        call().then_inc(T.sem[name], inc)
+        count[name] = count.get(name, 0) + inc
+        tok = (name, count[name])
+        snaps[tok] = dict(known[q])
+        for r in reads:
+            note(r, False, tok)
+        for r in writes:
+            note(r, True, tok)
+
+    def arrive(r, sem, val):
+        note(r, True, (sem, val))
+
+    def ready(q, reads):
+        wait(q, deps(reads, []))
+
+    return emit, arrive, ready, count
+
+
+def rank_program(g, core, T, topo):
+    rank = T.rank_of(core)
+    if rank is None:
+        return
+    emit, arrive, ready, count = make_tracker(g, T)
+    V, S, PE = g.vector, g.scalar, g.tensor
+
+    def R(n, lo, hi, st=1):
+        return (n, lo, hi, st)
+
+    def ap(r):
+        return T[r[0]][:, r[1]:r[2]] if r[3] == 1 else T[r[0]][:, r[1]:r[2]:r[3]]
+
+    def src(r, off):
+        return ap(r) if off is None else ap(r).indirect(ap(off))
+
+    def rd(*rs):
+        return [r for r in rs if isinstance(r, tuple)]
+
+    def val(x):
+        return ap(x) if isinstance(x, tuple) else x
+
+    def copy(out, in_, off=None):
+        emit("v", lambda: V.tensor_copy(ap(out), src(in_, off)), rd(in_, off), [out])
+
+    def ts(out, in_, s1, op0, s2=None, op1=None, off=None):
+        if op1 is None:
+            emit("v", lambda: V.tensor_scalar(ap(out), src(in_, off), val(s1), None, op0), rd(in_, off, s1), [out])
+        else:
+            emit("v", lambda: V.tensor_scalar(ap(out), src(in_, off), val(s1), val(s2), op0, op1), rd(in_, off, s1, s2), [out])
+
+    def tt(out, a, b, op, off=None):
+        emit("v", lambda: V.tensor_tensor(ap(out), src(a, off), ap(b), op), rd(a, b, off), [out])
+
+    def tr(out, in_):
+        emit("v", lambda: V.transpose(ap(out), ap(in_)), [in_], [out])
+
+    def ms(out, c):
+        emit("v", lambda: V.memset(ap(out), c), [], [out])
+
+    def qm(q, s, in_):
+        emit("v", lambda: V.quantize_mx(ap(q), ap(s), ap(in_)), [in_], [q, s])
+
+    def act(out, in_, off=None, scale=1.0):
+        func = AF.Identity if isinstance(scale, tuple) else AF.Copy
+        emit("s", lambda: S.activation(ap(out), src(in_, off), func, scale=val(scale)), rd(in_, off, scale), [out])
+
+    def mm(bank, n, w, ws, x, xs):
+        out = R("ps", 512 * bank, 512 * bank + n)
+        emit("t", lambda: PE.matmul_mx(ap(out), ap(w), ap(ws), ap(x), ap(xs), True, True), [w, ws, x, xs], [out])
+        return out
+
+    def load(q, out, in_ap, sem, code=False):
+        eng = {"y": g.sync, "s": g.scalar}[q]
+        emit(q, lambda: eng.dma_start(ap(out).bitcast(dt.uint8) if code else ap(out), in_ap), [], [out], sem, 16)
+
+    def iota(out, pattern, base, cm):
+        emit("g", lambda: g.iota(ap(out), pattern, base, cm, allow_small_or_imprecise_dtypes=True), [], [out])
+
+    load("s", R("tbi", 0, 22), T.pl[:], "ldp")
+    load("y", R("x0", 4 * F, 4 * C), T.x[:, 4 * F:4 * C], "ldx1")
+    load("s", R("tbi", 32, 54), T.dl[:], "ldd")
+    load("y", R("x0", 0, 4 * F), T.x[:, 0:4 * F], "ldx0")
+    load("s", R("tbi", 64, 86), T.kl[:], "ldk")
+    load("s", R("ut", 0, 512), T.u[:], "ldu")
+    load("y", R("wq", 0, 512), T.wc[:], "ldwc", True)
+    load("y", R("wp", 0, 512), T.ws[:], "ldws")
+    load("y", R("vt", 0, 512), T.v[:], "ldv")
+
+    ip = R("ci", 0, 1)
+    emit("g", lambda: g.iota(ap(ip), [[0, 1]], 0, 1), [], [ip])
+    iota(R("rc", 0, 5), [[0, 5]], 1000, 0)
+    iota(R("rc", 5, 17), [[0, 4], [32, 3]], 0, 0)
+    iota(R("rc", 16, 21), [[0, 5]], 1000, 0)
+    iota(R("rc", 21, 33), [[0, 4], [32, 3]], 0, 0)
+    iota(R("i2", 0, 22), [[2, 11], [0, 2]], 0, 0)
+    iota(R("gam", 0, 24), [[32, 12], [0, 2]], ROT - MID - 16, 0)
+    iota(R("gam", 24, 46), [[32, 11], [0, 2]], ROT - MID, 0)
+    ms(R("ones", 0, 512), 1.0)
+    for b in range(4):
+        e = R("eb", 512 * b, 512 * b + 512)
+        emit("g", lambda: g.affine_select(ap(e), ap(R("ones", 0, 512)), [[-1, 512]], AO.is_equal, 0.0, b, 4), [R("ones", 0, 512)], [e])
+    ms(R("tbs", 0, 256), 0.0)
+    ms(R("ttb", 0, 128), 0.0)
+    ms(R("tf", 352, 368), 0.0)
+    for n in ("gb", "gl", "wa", "wb"):
+        ms(R(n, 0, 16), 0.0)
+        ms(R(n, 368, 384), 0.0)
+    def cf(i):
+        return R("cf", i, i + 1)
+
+    def ci(i):
+        return R("ci", i, i + 1)
+    ts(ci(1), ip, 15, AO.bitwise_and)
+    ts(ci(2), ip, 4, AO.arith_shift_right, 1, AO.bitwise_and)
+    ts(ci(3), ip, 31, AO.bitwise_and)
+    tr(R("lc", 0, 32), R("rc", 0, 32))
+    copy(R("cf", 0, 3), R("ci", 1, 4))
+    tt(ci(4), ci(1), ci(2), AO.add)
+    q_, par, i32, l32, odd = cf(0), cf(1), cf(2), R("lc", 0, 1), cf(3)
+    ts(cf(4), par, 97.0, AO.mult)
+    ts(cf(5), par, -127.0, AO.mult, 128.0, AO.add)
+    ts(ci(5), ci(4), 1, AO.bitwise_and)
+    tt(cf(6), cf(4), l32, AO.add)
+    tt(cf(7), cf(5), l32, AO.add)
+    copy(odd, ci(5))
+    ts(cf(6), cf(6), 224.0, AO.min)
+    ts(cf(7), cf(7), 224.0, AO.min)
+    ts(R("offi", 0, 22, 2), R("i2", 0, 22, 2), cf(6), AO.add)
+    ts(R("offi", 1, 22, 2), R("i2", 1, 22, 2), cf(7), AO.add)
+    RM, THR = cf(8), cf(9)
+    ts(RM, l32, 500.0, AO.is_lt)
+    ts(THR, q_, 3.5, AO.is_ge, 1e28, AO.mult)
+
+    for m, s in ((0, "p"), (32, "d"), (64, "k")):
+        ts(R("tbs", m, m + 22), R("tbi", m, m + 22), float(-MID), AO.add)
+    copy(R("opi", 0, 22), R("tbi", 0, 22))
+    tr(R("ttb", 16, 112), R("tbs", 0, 96))
+    tr(R("tbs", 96, 224), R("ttb", 0, 128))
+    copy(R("tf", 0, 352), R("tbs", 0, 256), R("offi", 0, 22))
+    tr(R("wa", 16, 368), R("tf", 0, 352))
+    GAM = R("gam", 0, 46)
+    ts(GAM, GAM, i32, AO.add)
+
+    def sm(i):
+        return R("sm", 48 * i, 48 * i + 46)
+
+    def prelinks(off):
+        act(R("gl", 16, 368), R("wa", 16, 368), off)
+        return "gl"
+
+    def prelinks2():
+        tr(R("glt", 0, 384), R("gl", 0, 384))
+        tr(R("glt", 384, 736), R("gl", 16, 368))
+
+    def prelinks3():
+        tt(sm(2), R("glt", 5, 736, 16), R("glt", 6, 736, 16), AO.subtract)
+        tt(sm(0), R("glt", 6, 736, 16), GAM, AO.subtract)
+        ts(sm(1), sm(2), -352.0, AO.add)
+
+    prelinks(R("opi", 0, 22))
+    ts(cf(10), odd, -23.0, AO.mult, 24.0, AO.add)
+    ts(cf(14), odd, 23.0, AO.mult, 12.0, AO.add)
+    tt(cf(11), cf(10), q_, AO.add)
+    tt(cf(15), cf(14), q_, AO.add)
+    ts(cf(12), cf(11), 16.0, AO.add, 45.0, AO.min)
+    ts(cf(16), cf(15), 45.0, AO.min, 16.0, AO.mult)
+    copy(R("pk", 0, 2), R("cf", 11, 13))
+    ts(R("pk", 2, 4), R("cf", 11, 13), 16.0, AO.mult, 5.0, AO.add)
+    ts(R("pk", 4, 6), R("cf", 11, 13), 16.0, AO.mult, 7.0, AO.add)
+    ts(R("pk", 6, 7), cf(16), 7.0, AO.add)
+    PM, PP, PK, PK1, PO = R("pk", 0, 2), R("pk", 2, 4), R("pk", 4, 6), R("pk", 4, 5), R("pk", 6, 7)
+    ms(R("sm", 384, 432), 0.0)
+
+    def state_half(r, h):
+        lo, hi = (0, F) if h == 0 else (F, C)
+        qm(R("qx", lo, hi), R("sx", lo, hi), R("x%d" % r, 4 * lo, 4 * hi))
+
+    def signs_half(h):
+        lo, hi = (0, F) if h == 0 else (F, C)
+        out = mm(5 - h, F, R("qu", 0, 128), R("su", 0, 128), R("qx", lo, hi), R("sx", lo, hi))
+        ts(R("bt", lo, hi), out, THR, AO.is_gt)
+
+    def planes(r, h):
+        lo, hi = (0, F) if h == 0 else (F, C)
+        for t in range(4):
+            act(R("xp", C * t + lo, C * t + hi), R("x%d" % r, 4 * lo + t, 4 * hi, 4), scale=0.5)
+
+    state_half(0, 1)
+    qm(R("qu", 0, 128), R("su", 0, 128), R("ut", 0, 512))
+    planes(0, 1)
+    act(R("wa", 736, 1088), R("wa", 16, 368))
+    act(R("wb", 736, 1088), R("wa", 16, 368))
+    planes(0, 0)
+    prelinks2()
+    prelinks3()
+    state_half(0, 0)
+    tr(R("wa", 384, 736), R("tf", 1, 353))
+    signs_half(1)
+    signs_half(0)
+    ms(R("n1", 736, 752), 0.0)
+    ms(R("n2", 736, 752), 0.0)
+    ms(R("mf", 0, 16), 0.0)
+    ms(R("mo", 368, 384), 0.0)
+
+    ALL = R("wa", 16, 1088)
+    ALLB = R("wb", 16, 1088)
+
+    def turn(dst, srcb, a, b):
+        tr(R(dst, 384 + a, 384 + b), R(srcb, 16 + a, 16 + b))
+        e = 384 if b == C else b
+        tr(R(dst, a, e), R(srcb, a, e))
+
+    dst = T.cores[0]
+    offp = R("opi", 0, 22)
+    for r in range(3):
+        s = STEP[r]
+        source, target = T.cores[(rank - s) % 8], T.cores[(rank + s) % 8]
+        last = r == 2
+        n_half = len(topo.engines(core, source)) // 2
+        n_all = len(topo.engines(core, target))
+        arrive(R("pin%d" % r, 0, 22), "ap%d" % r, n_half)
+        arrive(R("kin%d" % r, 0, 22), "ak%d" % r, n_half)
+        arrive(R("qin%d" % r, 0, F), "ac%d" % r, n_all)
+        arrive(R("sin%d" % r, 0, F), "as%d" % r, n_all)
+        X, XN = "x%d" % r, "x%d" % (r + 1)
+
+        k = 10
+        a = 16 * k
+        BT = R("bt", 0, C)
+        copy(R("gb", 16, 16 + a), BT, R(offp[0], 0, k))
+        act(R("gb", 16 + a, 368), BT, R(offp[0], k, 22))
+        turn("gt", "gb", 0, a)
+        turn("gt", "gb", a, C)
+        A0, A1 = R("gt", 0, 736, 16), R("gt", 1, 736, 16)
+        tt(sm(3), A1, sm(1), AO.mult)
+        ts(sm(4), A1, 352.0, AO.mult)
+        tt(sm(5), sm(3), sm(0), AO.add)
+        tt(sm(6), sm(4), GAM, AO.add)
+        tt(sm(7), A0, sm(5), AO.mult)
+        tt(sm(8), sm(7), sm(6), AO.add)
+        ts(R("o1", 0, 32), R("sm", 48 * 8, 48 * 9), float(MID), AO.add, off=PM)
+        tt(R("wb", 16, 368), ALL, BT, AO.add, off=R("o1", 0, 22))
+        if r:
+            planes(r, 0)
+        turn("n1", "wb", 0, C)
+        ts(R("op1", 0, 32), R("n1", 0, 736), float(MID), AO.add, off=PP)
+
+        k = 8
+        a = 16 * k
+        CB = R("wb", 16, 368)
+        act(R("gb", 16 + a, 368), CB, R("op1", k, 22))
+        copy(R("gb", 16, 16 + a), CB, R("op1", 0, k))
+        turn("gt", "gb", 0, a)
+        tr(R("wb", 384, 736), R("n1", 385, 737))
+        turn("gt", "gb", a, C)
+        A2, A3, GP, GD = R("gt", 2, 736, 16), R("gt", 3, 736, 16), R("gt", 5, 736, 16), R("gt", 6, 736, 16)
+        tt(sm(3), GP, GD, AO.subtract)
+        ts(sm(4), A3, 352.0, AO.mult)
+        tt(sm(5), A3, sm(3), AO.mult)
+        tt(sm(6), sm(4), GAM, AO.add)
+        tt(sm(7), sm(5), GD, AO.add)
+        tt(sm(9), sm(7), sm(6), AO.subtract)
+        tt(sm(3), A2, sm(9), AO.mult)
+        tt(sm(8), sm(3), sm(6), AO.add)
+        ts(R("o2", 0, 32), R("sm", 48 * 8, 48 * 9), float(MID), AO.add, off=PM)
+        k = 10
+        a = 16 * k
+        act(R("wa", 16 + a, 368), ALLB, R("o2", k, 22), scale=RM)
+        ts(R("wa", 16, 16 + a), ALLB, RM, AO.mult, off=R("o2", 0, k))
+        turn("n2", "wa", 0, a)
+        turn("n2", "wa", a, C)
+        OP = "opn%d" % r
+        N2 = R("n2", 0, 736)
+        ts(R(OP, 0, 32), N2, float(MID), AO.add, off=PP)
+        KS = R("ks%d" % r, 0, 22)
+        copy(KS, R("n2", 384 + 7, 736, 16))
+        ts(R("ok", 0, 32), N2, float(MID), AO.add, off=PK)
+        offp = R(OP, 0, 22)
+
+        ready("g", [offp, KS])
+        trans = []
+        for d, sr, ds, sem, part in ((source, offp, R("pin%d" % r, 0, 22), "ap%d" % r, 0), (target, KS, R("kin%d" % r, 0, 22), "ak%d" % r, 1)):
+            rid, pid = topo.addr(d, core)
+            eng = topo.engines(core, d)
+            eng = eng[part * n_half:(part + 1) * n_half]
+            trans.append(RemoteDMATransfer(src=ap(sr), dst=ap(ds), dst_ids=[DstId(rid=rid, pnc=pid)],
+                                           dma_engine_mask=sum(1 << e for e in eng), remote_sem=T.sem[sem]))
+        g.remote_dma_fused(trans, local_sem=T.sem["sent"])
+        count["sent"] = count.get("sent", 0) + 2 * n_half
+
+        runs = ((0, 12), (12, 22))
+        for c, (k0, k1) in enumerate(runs):
+            lo, hi = 16 * k0, 16 * k1
+            if not last and c == 0:
+                tr(R("wa", 384, 736), R("n2", 385, 737))
+            if r == 0 and c == 0:
+                for b in (0,):
+                    qm(R("qe", 128 * b, 128 * b + 128), R("se", 128 * b, 128 * b + 128), R("eb", 512 * b, 512 * b + 512))
+            for t in range(4):
+                win = R("xp", C * t, C * t + C)
+                zp = R("zp", C * t + lo, C * t + hi)
+                act(zp, win, R(OP, k0, k1))
+                tt(R("zt", 4 * lo + t, 4 * hi, 4), win, zp, AO.add, off=R("ok", k0, k1))
+            qm(R("qz", lo, hi), R("sz", lo, hi), R("zt", 4 * lo, 4 * hi))
+            for b in range(4):
+                mm(4 * c + b, hi - lo, R("wq", 128 * b, 128 * b + 128), R("wp", 128 * b, 128 * b + 128), R("qz", lo, hi), R("sz", lo, hi))
+        act(R("mf", 16, 208), R("wa", 16, 368), R("pin%d" % r, 0, 12))
+
+        def evict(q, c, b):
+            lo, w = (0, 192) if c == 0 else (192, 160)
+            bank = 512 * (4 * c + b)
+            o, i = R("hp", C * b + lo, C * b + lo + w), R("ps", bank, bank + w)
+            if q == "s":
+                act(o, i, scale=0.03125)
+            else:
+                ts(o, i, 0.03125, AO.mult)
+        for b in range(4):
+            evict("s", 0, b)
+        turn("gt", "mf", 0, 192)
+        ts(R("om", 0, 16), R("gt", 0, 736), float(MID), AO.add, off=PK1)
+        for b in range(4):
+            evict("s", 1, b)
+            ft = R("ft", b, 4 * F, 4)
+            hw = R("hp", C * b, C * b + C)
+            if b < 3:
+                copy(ft, hw, R("om", 0, 11))
+            else:
+                act(ft, hw, R("om", 0, 11))
+        qm(R("qf%d" % r, 0, F), R("sf%d" % r, 0, F), R("ft", 0, 4 * F))
+
+        QF, SF = R("qf%d" % r, 0, F), R("sf%d" % r, 0, F)
+        ready("g", [QF, SF])
+        rid, pid = topo.addr(target, core)
+        m = topo.mask(core, target)
+        g.remote_dma(ap(R("qin%d" % r, 0, F)).bitcast(dt.uint8), ap(QF).bitcast(dt.uint8), T.sem["ac%d" % r], T.sem["sent"], pid, rid, m)
+        g.remote_dma(ap(R("sin%d" % r, 0, F)), ap(SF), T.sem["as%d" % r], T.sem["sent"], pid, rid, m)
+        count["sent"] += 2 * n_all
+
+        if r == 0:
+            for b in (1, 2, 3):
+                qm(R("qe", 128 * b, 128 * b + 128), R("se", 128 * b, 128 * b + 128), R("eb", 512 * b, 512 * b + 512))
+
+        copy(R("n1", 384 + 7, 736, 16), R("kin%d" % r, 0, 22))
+        tr(R("kr", 0, C), R("n1", 384, 736))
+        act(R("mo", 176, 368), R("kr", 0, C), R(OP, 10, 22))
+        if not last:
+            prelinks(offp)
+        tr(R("gt", 384 + 160, 736), R("mo", 176, 368))
+        tr(R("gt", 192, 384), R("mo", 192, 384))
+        ts(R("oo", 0, 16), R("gt", 0, 736), float(MID), AO.add, off=PO)
+        for t in range(4):
+            tt(R(XN, 4 * F + t, 4 * C, 4), R("hp", C * t, C * t + C), R(X, 4 * F + t, 4 * C, 4), AO.add, off=R("oo", 0, 11))
+        state_half(r + 1, 1)
+        if not last:
+            planes(r + 1, 1)
+            prelinks2()
+            signs_half(1)
+        else:
+            qm(R("qv", 0, 128), R("sv", 0, 128), R("vt", 0, 512))
+            store(g, T, emit, ap, R, mm, act, ts, 1)
+            lkt = R("lkt", 0, C)
+            ts(lkt, R("wa", 16, 368), float(MID), AO.add)
+            for gr in range(8):
+                emit("y", lambda: g.sync.dma_start(T.lk[gr:gr + 1, :], T.lkt[16 * gr + 5:16 * gr + 8, :]), [lkt], [], "sty", 16)
+
+        for b in range(4):
+            out = mm(b, F, R("qe", 128 * b, 128 * b + 128), R("se", 128 * b, 128 * b + 128), R("qin%d" % r, 0, F), R("sin%d" % r, 0, F))
+            tt(R(XN, b, 4 * F, 4), out, R(X, b, 4 * F, 4), AO.add)
+        state_half(r + 1, 0)
+        if not last:
+            prelinks3()
+            signs_half(0)
+        else:
+            store(g, T, emit, ap, R, mm, act, ts, 0)
+
+    for n in ("cv", "cs", "ct", "cg", "sent", "sty", "sta"):
+        if count.get(n):
+            g.wait_ge(T.sem[n], count[n])
+
+
+def store(g, T, emit, ap, R, mm, act, ts, h):
+    lo, hi = (0, F) if h == 0 else (F, C)
+    Q, P, Y = R("qx", lo, hi), R("sx", lo, hi), R("yt", lo, hi)
+    out = mm(5 - h, F, R("qv", 0, 128), R("sv", 0, 128), Q, P)
+    emit("y", lambda: g.sync.dma_start(T.oc[:, 4 * lo:4 * hi], ap(Q).bitcast(dt.uint8)), [Q], [], "sty", 16)
+    for k in range(4):
+        q, e, sem = ("s", g.scalar, "sta") if k % 2 else ("y", g.sync, "sty")
+        emit(q, lambda: e.dma_start(T.osc[4 * k:4 * k + 4, lo:hi], T.sx[32 * k:32 * k + 4, lo:hi]), [P], [], sem, 16)
+    if h:
+        act(Y, out)
+    else:
+        ts(Y, out, 1.0, AO.mult)
+    emit("y", lambda: g.sync.dma_start(T.y[:, lo:hi], ap(Y)), [Y], [], "sty", 16)

@@ -1,4 +1,3 @@
-from concourse.bass import DstId, RemoteDMATransfer
 from concourse.mybir import dt, AluOpType as AO, ActivationFunctionType as AF
 
 C, F = 352, 176
@@ -11,7 +10,7 @@ SCRATCH = {
     "tbi": ("sbuf", [128, 96], I32), "tbs": ("sbuf", [128, 256], B16), "ttb": ("sbuf", [128, 128], B16), "tf": ("sbuf", [128, 368], B16),
     "ones": ("sbuf", [128, 512], B16), "eb": ("sbuf", [128, 2048], B16), "qe": ("sbuf", [128, 512], MXC), "se": ("sbuf", [128, 512], U8),
     "ci": ("sbuf", [128, 16], I32), "cf": ("sbuf", [128, 64], F32), "rc": ("sbuf", [128, 40], F32), "lc": ("sbuf", [128, 32], F32),
-    "i2": ("sbuf", [128, 24], F32), "gam": ("sbuf", [128, 48], F32), "offi": ("sbuf", [128, 24], U16), "pk": ("sbuf", [128, 8], U16),
+    "i2": ("sbuf", [128, 24], F32), "gam": ("sbuf", [128, 48], F32), "offi": ("sbuf", [128, 24], U16), "pk": ("sbuf", [128, 16], U16),
     "wq": ("sbuf", [128, 512], MXC), "wp": ("sbuf", [128, 512], U8),
     "ut": ("sbuf", [128, 512], B16), "qu": ("sbuf", [128, 128], MXC), "su": ("sbuf", [128, 128], U8),
     "vt": ("sbuf", [128, 512], B16), "qv": ("sbuf", [128, 128], MXC), "sv": ("sbuf", [128, 128], U8),
@@ -19,7 +18,7 @@ SCRATCH = {
     "xp": ("sbuf", [128, 4 * C], B16), "hp": ("sbuf", [128, 4 * C], B16), "zp": ("sbuf", [128, 4 * C], B16), "zt": ("sbuf", [128, 4 * C], B16),
     "ft": ("sbuf", [128, 4 * F], B16),
     "qx": ("sbuf", [128, C], MXC), "sx": ("sbuf", [128, C], U8), "qz": ("sbuf", [128, C], MXC), "sz": ("sbuf", [128, C], U8),
-    "bt": ("sbuf", [128, C], B16), "wa": ("sbuf", [128, 1088], B16), "wb": ("sbuf", [128, 1088], B16),
+    "bt": ("sbuf", [128, C], B16), "wr": ("sbuf", [128, 1408], B16), "td": ("sbuf", [128, 32], U16), "tp": ("sbuf", [128, 32], U16), "wa": ("sbuf", [128, 1792], B16), "wb": ("sbuf", [128, 1088], B16),
     "gb": ("sbuf", [128, 384], B16), "gl": ("sbuf", [128, 384], B16), "mf": ("sbuf", [128, 384], B16), "mo": ("sbuf", [128, 384], B16),
     "gt": ("sbuf", [128, 752], B16), "glt": ("sbuf", [128, 752], B16), "n1": ("sbuf", [128, 752], B16), "n2": ("sbuf", [128, 752], B16),
     "kr": ("sbuf", [128, C], B16), "sm": ("sbuf", [128, 480], F32),
@@ -153,7 +152,10 @@ def rank_program(g, core, T, topo):
     def qm(q, s, in_):
         emit("v", lambda: V.quantize_mx(ap(q), ap(s), ap(in_)), [in_], [q, s])
 
-    def act(out, in_, off=None, scale=1.0):
+    def act(out, in_, off=None, scale=1.0, bias=None):
+        if bias is not None:
+            emit("s", lambda: S.activation(ap(out), src(in_, off), AF.Identity, bias=ap(bias)), rd(in_, off, bias), [out])
+            return
         func = AF.Identity if isinstance(scale, tuple) else AF.Copy
         emit("s", lambda: S.activation(ap(out), src(in_, off), func, scale=val(scale)), rd(in_, off, scale), [out])
 
@@ -171,9 +173,9 @@ def rank_program(g, core, T, topo):
 
     load("s", R("tbi", 0, 22), T.pl[:], "ldp")
     load("y", R("x0", 4 * F, 4 * C), T.x[:, 4 * F:4 * C], "ldx1")
-    load("s", R("tbi", 32, 54), T.dl[:], "ldd")
+    load("s", R("tbi", 22, 44), T.dl[:], "ldd")
     load("y", R("x0", 0, 4 * F), T.x[:, 0:4 * F], "ldx0")
-    load("s", R("tbi", 64, 86), T.kl[:], "ldk")
+    load("s", R("tbi", 44, 66), T.kl[:], "ldk")
     load("s", R("ut", 0, 512), T.u[:], "ldu")
     load("y", R("wq", 0, 512), T.wc[:], "ldwc", True)
     load("y", R("wp", 0, 512), T.ws[:], "ldws")
@@ -182,22 +184,23 @@ def rank_program(g, core, T, topo):
     ip = R("ci", 0, 1)
     emit("g", lambda: g.iota(ap(ip), [[0, 1]], 0, 1), [], [ip])
     iota(R("rc", 0, 5), [[0, 5]], 1000, 0)
-    iota(R("rc", 5, 17), [[0, 4], [32, 3]], 0, 0)
+    iota(R("rc", 5, 17), [[0, 4], [22, 3]], 0, 0)
     iota(R("rc", 16, 21), [[0, 5]], 1000, 0)
-    iota(R("rc", 21, 33), [[0, 4], [32, 3]], 0, 0)
+    iota(R("rc", 21, 33), [[0, 4], [22, 3]], 0, 0)
     iota(R("i2", 0, 22), [[2, 11], [0, 2]], 0, 0)
-    iota(R("gam", 0, 24), [[32, 12], [0, 2]], ROT - MID - 16, 0)
-    iota(R("gam", 24, 46), [[32, 11], [0, 2]], ROT - MID, 0)
-    ms(R("ones", 0, 512), 1.0)
+    iota(R("gam", 0, 24), [[32, 12], [0, 2]], ROT + 176 - 16, 0)
+    iota(R("gam", 24, 46), [[32, 11], [0, 2]], ROT + 176, 0)
+    iota(R("ones", 0, 512), [[0, 512]], 1, 0)
     for b in range(4):
         e = R("eb", 512 * b, 512 * b + 512)
         emit("g", lambda: g.affine_select(ap(e), ap(R("ones", 0, 512)), [[-1, 512]], AO.is_equal, 0.0, b, 4), [R("ones", 0, 512)], [e])
-    ms(R("tbs", 0, 256), 0.0)
-    ms(R("ttb", 0, 128), 0.0)
-    ms(R("tf", 352, 368), 0.0)
-    for n in ("gb", "gl", "wa", "wb"):
-        ms(R(n, 0, 16), 0.0)
-        ms(R(n, 368, 384), 0.0)
+    ms(R("tbs", 224, 256), 0.0)
+    ms(R("tbs", 66, 96), 0.0)
+    for n, a in (("ttb", 0), ("ttb", 112), ("tf", 352), ("gl", 0), ("gl", 368), ("wa", 0), ("wa", 368), ("wb", 0), ("wb", 368),
+                 ("gb", 0), ("gb", 368), ("n1", 736), ("n2", 736), ("mf", 0), ("mo", 368)):
+        act(R(n, a, a + 16), R("tbs", 224, 240))
+    act(R("sm", 384, 400), R("tbs", 224, 240))
+    act(R("sm", 400, 432), R("tbs", 224, 256))
     def cf(i):
         return R("cf", i, i + 1)
 
@@ -220,82 +223,97 @@ def rank_program(g, core, T, topo):
     ts(cf(7), cf(7), 224.0, AO.min)
     ts(R("offi", 0, 22, 2), R("i2", 0, 22, 2), cf(6), AO.add)
     ts(R("offi", 1, 22, 2), R("i2", 1, 22, 2), cf(7), AO.add)
-    RM, THR = cf(8), cf(9)
-    ts(RM, l32, 500.0, AO.is_lt)
-    ts(THR, q_, 3.5, AO.is_ge, 1e28, AO.mult)
+    RM, THR, WT, NB = cf(8), cf(9), cf(19), cf(20)
 
-    for m, s in ((0, "p"), (32, "d"), (64, "k")):
-        ts(R("tbs", m, m + 22), R("tbi", m, m + 22), float(-MID), AO.add)
+    ts(R("tbs", 0, 66), R("tbi", 0, 66), float(-MID), AO.add)
     copy(R("opi", 0, 22), R("tbi", 0, 22))
     tr(R("ttb", 16, 112), R("tbs", 0, 96))
     tr(R("tbs", 96, 224), R("ttb", 0, 128))
     copy(R("tf", 0, 352), R("tbs", 0, 256), R("offi", 0, 22))
     tr(R("wa", 16, 368), R("tf", 0, 352))
     GAM = R("gam", 0, 46)
-    ts(GAM, GAM, i32, AO.add)
 
     def sm(i):
         return R("sm", 48 * i, 48 * i + 46)
 
+    PM, PP, PK, PK1, PO, PD = R("pk", 0, 2), R("pk", 2, 4), R("pk", 4, 6), R("pk", 4, 5), R("pk", 6, 7), R("pk", 8, 10)
+
     def prelinks(off):
         act(R("gl", 16, 368), R("wa", 16, 368), off)
-        return "gl"
 
     def prelinks2():
         tr(R("glt", 0, 384), R("gl", 0, 384))
         tr(R("glt", 384, 736), R("gl", 16, 368))
 
     def prelinks3():
-        tt(sm(2), R("glt", 5, 736, 16), R("glt", 6, 736, 16), AO.subtract)
-        tt(sm(0), R("glt", 6, 736, 16), GAM, AO.subtract)
-        ts(sm(1), sm(2), -352.0, AO.add)
+        for o, pick, a in (("td", PD, 1088), ("tp", PP, 1440)):
+            ts(R(o, 0, 32), R("glt", 0, 736), float(MID), AO.add, off=pick)
+            act(R("wa", a, a + C), R("wa", 16, 368), R(o, 0, 22))
+
+    def prelinks4():
+        act(R("wr", 704, 1056), R("wa", 384, 736), R("td", 0, 22))
+        act(R("wr", 1056, 1408), R("wa", 384, 736), R("tp", 0, 22))
 
     prelinks(R("opi", 0, 22))
+    act(R("wa", 736, 1088), R("wa", 16, 368))
     ts(cf(10), odd, -23.0, AO.mult, 24.0, AO.add)
-    ts(cf(14), odd, 23.0, AO.mult, 12.0, AO.add)
+    ts(THR, q_, 3.5, AO.is_ge, 1e28, AO.mult)
+    ts(cf(17), q_, 0.0, AO.is_equal, 352.0, AO.mult)
+    ts(cf(18), q_, 2.0, AO.is_equal, 1696.0, AO.mult)
     tt(cf(11), cf(10), q_, AO.add)
-    tt(cf(15), cf(14), q_, AO.add)
+    ts(WT, cf(17), cf(18), AO.add, 352.0, AO.add)
     ts(cf(12), cf(11), 16.0, AO.add, 45.0, AO.min)
-    ts(cf(16), cf(15), 45.0, AO.min, 16.0, AO.mult)
-    copy(R("pk", 0, 2), R("cf", 11, 13))
-    ts(R("pk", 2, 4), R("cf", 11, 13), 16.0, AO.mult, 5.0, AO.add)
-    ts(R("pk", 4, 6), R("cf", 11, 13), 16.0, AO.mult, 7.0, AO.add)
-    ts(R("pk", 6, 7), cf(16), 7.0, AO.add)
-    PM, PP, PK, PK1, PO = R("pk", 0, 2), R("pk", 2, 4), R("pk", 4, 6), R("pk", 4, 5), R("pk", 6, 7)
-    ms(R("sm", 384, 432), 0.0)
+    ts(PP, R("cf", 11, 13), 16.0, AO.mult, 5.0, AO.add)
+    ts(PD, R("cf", 11, 13), 16.0, AO.mult, 6.0, AO.add)
+    copy(PM, R("cf", 11, 13))
+    rest = [
+        lambda: ts(GAM, GAM, i32, AO.add),
+        lambda: ts(cf(21), q_, 2.0, AO.is_equal, -1024.0, AO.mult),
+        lambda: ts(cf(22), q_, 3.0, AO.is_equal, -176.0, AO.mult),
+        lambda: tt(NB, cf(21), cf(22), AO.add),
+        lambda: ts(RM, l32, 500.0, AO.is_lt),
+        lambda: ts(PK, R("cf", 11, 13), 16.0, AO.mult, 7.0, AO.add),
+        lambda: ts(cf(14), odd, 23.0, AO.mult, 12.0, AO.add),
+        lambda: ms(cf(23), float(MID)),
+        lambda: tt(cf(15), cf(14), q_, AO.add),
+        lambda: ts(cf(16), cf(15), 45.0, AO.min, 16.0, AO.mult),
+        lambda: ts(PO, cf(16), 7.0, AO.add),
+    ]
+
+    def fill(n):
+        for i in range(n):
+            if rest:
+                rest.pop(0)()
 
     def state_half(r, h):
         lo, hi = (0, F) if h == 0 else (F, C)
         qm(R("qx", lo, hi), R("sx", lo, hi), R("x%d" % r, 4 * lo, 4 * hi))
 
-    def signs_half(h):
+    def signs_mm(h):
         lo, hi = (0, F) if h == 0 else (F, C)
-        out = mm(5 - h, F, R("qu", 0, 128), R("su", 0, 128), R("qx", lo, hi), R("sx", lo, hi))
-        ts(R("bt", lo, hi), out, THR, AO.is_gt)
+        mm(5 - h, F, R("qu", 0, 128), R("su", 0, 128), R("qx", lo, hi), R("sx", lo, hi))
+
+    def signs_ts(h):
+        lo, hi = (0, F) if h == 0 else (F, C)
+        ts(R("bt", lo, hi), R("ps", 512 * (5 - h), 512 * (5 - h) + F), THR, AO.is_gt, WT, AO.mult)
 
     def planes(r, h):
         lo, hi = (0, F) if h == 0 else (F, C)
         for t in range(4):
             act(R("xp", C * t + lo, C * t + hi), R("x%d" % r, 4 * lo + t, 4 * hi, 4), scale=0.5)
 
-    state_half(0, 1)
-    qm(R("qu", 0, 128), R("su", 0, 128), R("ut", 0, 512))
-    planes(0, 1)
-    act(R("wa", 736, 1088), R("wa", 16, 368))
-    act(R("wb", 736, 1088), R("wa", 16, 368))
-    planes(0, 0)
     prelinks2()
     prelinks3()
+    state_half(0, 1)
+    qm(R("qu", 0, 128), R("su", 0, 128), R("ut", 0, 512))
     state_half(0, 0)
     tr(R("wa", 384, 736), R("tf", 1, 353))
-    signs_half(1)
-    signs_half(0)
-    ms(R("n1", 736, 752), 0.0)
-    ms(R("n2", 736, 752), 0.0)
-    ms(R("mf", 0, 16), 0.0)
-    ms(R("mo", 368, 384), 0.0)
+    signs_mm(1)
+    signs_mm(0)
+    signs_ts(1)
+    signs_ts(0)
 
-    ALL = R("wa", 16, 1088)
+    ALL = R("wa", 384, 1792)
     ALLB = R("wb", 16, 1088)
 
     def turn(dst, srcb, a, b):
@@ -309,10 +327,10 @@ def rank_program(g, core, T, topo):
         s = STEP[r]
         source, target = T.cores[(rank - s) % 8], T.cores[(rank + s) % 8]
         last = r == 2
-        n_half = len(topo.engines(core, source)) // 2
         n_all = len(topo.engines(core, target))
-        arrive(R("pin%d" % r, 0, 22), "ap%d" % r, n_half)
-        arrive(R("kin%d" % r, 0, 22), "ak%d" % r, n_half)
+        PIN = R("pin%d" % r, 0, 12)
+        arrive(PIN, "ap%d" % r, len(topo.engines(source, core)))
+        arrive(R("kin%d" % r, 0, 22), "ak%d" % r, n_all)
         arrive(R("qin%d" % r, 0, F), "ac%d" % r, n_all)
         arrive(R("sin%d" % r, 0, F), "as%d" % r, n_all)
         X, XN = "x%d" % r, "x%d" % (r + 1)
@@ -325,43 +343,53 @@ def rank_program(g, core, T, topo):
         turn("gt", "gb", 0, a)
         turn("gt", "gb", a, C)
         A0, A1 = R("gt", 0, 736, 16), R("gt", 1, 736, 16)
-        tt(sm(3), A1, sm(1), AO.mult)
-        ts(sm(4), A1, 352.0, AO.mult)
-        tt(sm(5), sm(3), sm(0), AO.add)
-        tt(sm(6), sm(4), GAM, AO.add)
-        tt(sm(7), A0, sm(5), AO.mult)
-        tt(sm(8), sm(7), sm(6), AO.add)
-        ts(R("o1", 0, 32), R("sm", 48 * 8, 48 * 9), float(MID), AO.add, off=PM)
+        tt(sm(3), A0, A1, AO.add)
+        fill(1)
+        tt(sm(8), sm(3), GAM, AO.add)
+        fill(1)
+        ts(R("o1", 0, 32), R("sm", 48 * 8, 48 * 9), float(-ROT - 176), AO.add, off=PM)
+        fill(1)
         tt(R("wb", 16, 368), ALL, BT, AO.add, off=R("o1", 0, 22))
-        if r:
-            planes(r, 0)
+        if r == 0:
+            act(R("wb", 736, 1088), R("wa", 736, 1088))
+            planes(0, 1)
+        else:
+            act(R("wb", 384, 736), R("wr", 0, 1408), R("o1", 0, 22))
+        planes(r, 0)
+        fill(1)
         turn("n1", "wb", 0, C)
+        fill(1)
         ts(R("op1", 0, 32), R("n1", 0, 736), float(MID), AO.add, off=PP)
+        fill(1)
 
-        k = 8
+        k = 8 if r == 0 else 10
         a = 16 * k
         CB = R("wb", 16, 368)
-        act(R("gb", 16 + a, 368), CB, R("op1", k, 22))
-        copy(R("gb", 16, 16 + a), CB, R("op1", 0, k))
+        act(R("gb", 16 + a, 368), CB, R("op1", k, 22), bias=NB)
+        ts(R("gb", 16, 16 + a), CB, NB, AO.add, off=R("op1", 0, k))
         turn("gt", "gb", 0, a)
-        tr(R("wb", 384, 736), R("n1", 385, 737))
+        if r == 0:
+            tr(R("wb", 384, 736), R("n1", 385, 737))
         turn("gt", "gb", a, C)
         A2, A3, GP, GD = R("gt", 2, 736, 16), R("gt", 3, 736, 16), R("gt", 5, 736, 16), R("gt", 6, 736, 16)
-        tt(sm(3), GP, GD, AO.subtract)
-        ts(sm(4), A3, 352.0, AO.mult)
-        tt(sm(5), A3, sm(3), AO.mult)
-        tt(sm(6), sm(4), GAM, AO.add)
-        tt(sm(7), sm(5), GD, AO.add)
-        tt(sm(9), sm(7), sm(6), AO.subtract)
-        tt(sm(3), A2, sm(9), AO.mult)
-        tt(sm(8), sm(3), sm(6), AO.add)
-        ts(R("o2", 0, 32), R("sm", 48 * 8, 48 * 9), float(MID), AO.add, off=PM)
+        tt(sm(1), GP, A3, AO.add)
+        tt(sm(2), GD, A3, AO.subtract)
+        tt(sm(3), GAM, A3, AO.add)
+        tt(sm(4), sm(1), sm(2), AO.max)
+        tt(sm(5), sm(3), A2, AO.subtract)
+        tt(sm(6), sm(4), A2, AO.add)
+        fill(1)
+        tt(sm(8), sm(6), sm(5), AO.max)
+        fill(1)
+        ts(R("o2", 0, 32), R("sm", 48 * 8, 48 * 9), -1024.0, AO.add, off=PM)
+        fill(1)
         k = 10
         a = 16 * k
         act(R("wa", 16 + a, 368), ALLB, R("o2", k, 22), scale=RM)
         ts(R("wa", 16, 16 + a), ALLB, RM, AO.mult, off=R("o2", 0, k))
         turn("n2", "wa", 0, a)
         turn("n2", "wa", a, C)
+        fill(1)
         OP = "opn%d" % r
         N2 = R("n2", 0, 736)
         ts(R(OP, 0, 32), N2, float(MID), AO.add, off=PP)
@@ -370,25 +398,17 @@ def rank_program(g, core, T, topo):
         ts(R("ok", 0, 32), N2, float(MID), AO.add, off=PK)
         offp = R(OP, 0, 22)
 
-        ready("g", [offp, KS])
-        trans = []
-        for d, sr, ds, sem, part in ((source, offp, R("pin%d" % r, 0, 22), "ap%d" % r, 0), (target, KS, R("kin%d" % r, 0, 22), "ak%d" % r, 1)):
+        for d, sr, ds, sem in ((source, R(OP, 0, 12), PIN, "ap%d" % r), (target, KS, R("kin%d" % r, 0, 22), "ak%d" % r)):
+            ready("g", [sr])
             rid, pid = topo.addr(d, core)
-            eng = topo.engines(core, d)
-            eng = eng[part * n_half:(part + 1) * n_half]
-            trans.append(RemoteDMATransfer(src=ap(sr), dst=ap(ds), dst_ids=[DstId(rid=rid, pnc=pid)],
-                                           dma_engine_mask=sum(1 << e for e in eng), remote_sem=T.sem[sem]))
-        g.remote_dma_fused(trans, local_sem=T.sem["sent"])
-        count["sent"] = count.get("sent", 0) + 2 * n_half
+            g.remote_dma(ap(ds), ap(sr), T.sem[sem], T.sem["sent"], pid, rid, topo.mask(core, d))
+            count["sent"] = count.get("sent", 0) + len(topo.engines(core, d))
 
-        runs = ((0, 12), (12, 22))
-        for c, (k0, k1) in enumerate(runs):
+        if not last:
+            tr(R("wa", 384, 736), R("n2", 385, 737))
+        fill(20)
+        for c, (k0, k1) in enumerate(((0, 12), (12, 22))):
             lo, hi = 16 * k0, 16 * k1
-            if not last and c == 0:
-                tr(R("wa", 384, 736), R("n2", 385, 737))
-            if r == 0 and c == 0:
-                for b in (0,):
-                    qm(R("qe", 128 * b, 128 * b + 128), R("se", 128 * b, 128 * b + 128), R("eb", 512 * b, 512 * b + 512))
             for t in range(4):
                 win = R("xp", C * t, C * t + C)
                 zp = R("zp", C * t + lo, C * t + hi)
@@ -397,22 +417,25 @@ def rank_program(g, core, T, topo):
             qm(R("qz", lo, hi), R("sz", lo, hi), R("zt", 4 * lo, 4 * hi))
             for b in range(4):
                 mm(4 * c + b, hi - lo, R("wq", 128 * b, 128 * b + 128), R("wp", 128 * b, 128 * b + 128), R("qz", lo, hi), R("sz", lo, hi))
-        act(R("mf", 16, 208), R("wa", 16, 368), R("pin%d" % r, 0, 12))
 
-        def evict(q, c, b):
+        def evict(c, b):
             lo, w = (0, 192) if c == 0 else (192, 160)
             bank = 512 * (4 * c + b)
-            o, i = R("hp", C * b + lo, C * b + lo + w), R("ps", bank, bank + w)
-            if q == "s":
-                act(o, i, scale=0.03125)
-            else:
-                ts(o, i, 0.03125, AO.mult)
-        for b in range(4):
-            evict("s", 0, b)
+            act(R("hp", C * b + lo, C * b + lo + w), R("ps", bank, bank + w), scale=0.03125)
+
+        for b in range(3):
+            evict(0, b)
+        act(R("mf", 16, 208), R("wa", 16, 368), R("pin%d" % r, 0, 12))
+        evict(0, 3)
+        if r == 0:
+            for b in range(4):
+                qm(R("qe", 128 * b, 128 * b + 128), R("se", 128 * b, 128 * b + 128), R("eb", 512 * b, 512 * b + 512))
+        if r == 1:
+            qm(R("qv", 0, 128), R("sv", 0, 128), R("vt", 0, 512))
         turn("gt", "mf", 0, 192)
         ts(R("om", 0, 16), R("gt", 0, 736), float(MID), AO.add, off=PK1)
         for b in range(4):
-            evict("s", 1, b)
+            evict(1, b)
             ft = R("ft", b, 4 * F, 4)
             hw = R("hp", C * b, C * b + C)
             if b < 3:
@@ -429,15 +452,14 @@ def rank_program(g, core, T, topo):
         g.remote_dma(ap(R("sin%d" % r, 0, F)), ap(SF), T.sem["as%d" % r], T.sem["sent"], pid, rid, m)
         count["sent"] += 2 * n_all
 
-        if r == 0:
-            for b in (1, 2, 3):
-                qm(R("qe", 128 * b, 128 * b + 128), R("se", 128 * b, 128 * b + 128), R("eb", 512 * b, 512 * b + 512))
-
+        if not last:
+            prelinks(offp)
         copy(R("n1", 384 + 7, 736, 16), R("kin%d" % r, 0, 22))
         tr(R("kr", 0, C), R("n1", 384, 736))
         act(R("mo", 176, 368), R("kr", 0, C), R(OP, 10, 22))
         if not last:
-            prelinks(offp)
+            prelinks2()
+            prelinks3()
         tr(R("gt", 384 + 160, 736), R("mo", 176, 368))
         tr(R("gt", 192, 384), R("mo", 192, 384))
         ts(R("oo", 0, 16), R("gt", 0, 736), float(MID), AO.add, off=PO)
@@ -446,13 +468,15 @@ def rank_program(g, core, T, topo):
         state_half(r + 1, 1)
         if not last:
             planes(r + 1, 1)
-            prelinks2()
-            signs_half(1)
+            prelinks4()
+            signs_mm(1)
+            tr(R("wr", 0, 352), R("n2", 386, 738))
+            if r == 0:
+                tr(R("wr", 352, 704), R("tf", 1, 353))
         else:
-            qm(R("qv", 0, 128), R("sv", 0, 128), R("vt", 0, 512))
             store(g, T, emit, ap, R, mm, act, ts, 1)
             lkt = R("lkt", 0, C)
-            ts(lkt, R("wa", 16, 368), float(MID), AO.add)
+            act(lkt, R("wa", 16, 368), bias=cf(23))
             for gr in range(8):
                 emit("y", lambda: g.sync.dma_start(T.lk[gr:gr + 1, :], T.lkt[16 * gr + 5:16 * gr + 8, :]), [lkt], [], "sty", 16)
 
@@ -461,8 +485,9 @@ def rank_program(g, core, T, topo):
             tt(R(XN, b, 4 * F, 4), out, R(X, b, 4 * F, 4), AO.add)
         state_half(r + 1, 0)
         if not last:
-            prelinks3()
-            signs_half(0)
+            signs_ts(1)
+            signs_mm(0)
+            signs_ts(0)
         else:
             store(g, T, emit, ap, R, mm, act, ts, 0)
 

from concourse.mybir import dt, AluOpType as AO, ActivationFunctionType as AF

C, F = 352, 176
STEP = [2, 4, 1]
MID = 176
ROT, DRAWN = 368, 720
B16, F32, I32, U16, U8, MXC = "bfloat16", "float32", "int32", "uint16", "uint8", "float8_e4m3fn_x4"

SCRATCH = {
    "tbi": ("sbuf", [128, 96], I32), "tbs": ("sbuf", [128, 256], B16), "ttb": ("sbuf", [128, 128], B16), "tf": ("sbuf", [128, 368], B16),
    "ones": ("sbuf", [128, 512], B16), "eb": ("sbuf", [128, 2048], B16), "qe": ("sbuf", [128, 512], MXC), "se": ("sbuf", [128, 512], U8),
    "ci": ("sbuf", [128, 16], I32), "cf": ("sbuf", [128, 64], F32), "rc": ("sbuf", [128, 40], F32), "lc": ("sbuf", [128, 32], F32),
    "i2": ("sbuf", [128, 24], F32), "gam": ("sbuf", [128, 48], F32), "offi": ("sbuf", [128, 24], U16), "pk": ("sbuf", [128, 16], U16),
    "wq": ("sbuf", [128, 512], MXC), "wp": ("sbuf", [128, 512], U8),
    "ut": ("sbuf", [128, 512], B16), "qu": ("sbuf", [128, 128], MXC), "su": ("sbuf", [128, 128], U8),
    "vt": ("sbuf", [128, 512], B16), "qv": ("sbuf", [128, 128], MXC), "sv": ("sbuf", [128, 128], U8),
    "x0": ("sbuf", [128, 4 * C], B16), "x1": ("sbuf", [128, 4 * C], B16), "x2": ("sbuf", [128, 4 * C], B16), "x3": ("sbuf", [128, 4 * C], B16),
    "xp": ("sbuf", [128, 4 * C], B16), "hp": ("sbuf", [128, 4 * C], B16), "zp": ("sbuf", [128, 4 * C], B16), "zt": ("sbuf", [128, 4 * C], B16),
    "ft": ("sbuf", [128, 4 * F], B16),
    "qx": ("sbuf", [128, C], MXC), "sx": ("sbuf", [128, C], U8), "qz": ("sbuf", [128, C], MXC), "sz": ("sbuf", [128, C], U8),
    "bt": ("sbuf", [128, C], B16), "wr": ("sbuf", [128, 1408], B16), "td": ("sbuf", [128, 32], U16), "tp": ("sbuf", [128, 32], U16), "wa": ("sbuf", [128, 1792], B16), "wb": ("sbuf", [128, 1088], B16),
    "gb": ("sbuf", [128, 384], B16), "gl": ("sbuf", [128, 384], B16), "mf": ("sbuf", [128, 384], B16), "mo": ("sbuf", [128, 384], B16),
    "gt": ("sbuf", [128, 752], B16), "glt": ("sbuf", [128, 752], B16), "n1": ("sbuf", [128, 752], B16), "n2": ("sbuf", [128, 752], B16),
    "kr": ("sbuf", [128, C], B16), "sm": ("sbuf", [128, 480], F32),
    "o1": ("sbuf", [128, 32], U16), "o2": ("sbuf", [128, 32], U16), "op1": ("sbuf", [128, 32], U16), "ok": ("sbuf", [128, 32], U16),
    "opi": ("sbuf", [128, 32], U16), "om": ("sbuf", [128, 16], U16), "oo": ("sbuf", [128, 16], U16),
    "lkt": ("sbuf", [128, C], F32), "yt": ("sbuf", [128, C], F32),
    "ps": ("psum", [128, 4096], F32),
}
for _r in range(3):
    SCRATCH["opn%d" % _r] = ("sbuf", [128, 32], U16)
    SCRATCH["ks%d" % _r] = ("sbuf", [128, 22], B16)
    SCRATCH["pin%d" % _r] = ("sbuf", [128, 22], U16)
    SCRATCH["kin%d" % _r] = ("sbuf", [128, 22], B16)
    SCRATCH["qf%d" % _r] = ("sbuf", [128, F], MXC)
    SCRATCH["sf%d" % _r] = ("sbuf", [128, F], U8)
    SCRATCH["qin%d" % _r] = ("sbuf", [128, F], MXC)
    SCRATCH["sin%d" % _r] = ("sbuf", [128, F], U8)
SEMAPHORES = ["cv", "cs", "ct", "cg", "sent", "sty", "sta",
              "ldp", "ldd", "ldk", "ldx0", "ldx1", "ldu", "ldv", "ldwc", "ldws"]
SEMAPHORES += [k + str(r) for r in range(3) for k in ("ap", "ak", "ac", "as")]


def make_tracker(g, T):
    queues = {"v": g.vector, "s": g.scalar, "t": g.tensor, "g": g, "y": g.sync}
    own = {"v": "cv", "s": "cs", "t": "ct", "g": "cg"}
    count = {}
    known = {q: {} for q in queues}
    snaps = {}
    hist = {}

    def span(r):
        n, lo, hi, st = r
        return (n, lo // 512 * 512, (hi + 511) // 512 * 512, 1) if n == "ps" else r

    def meet(a, b):
        if a[1] >= b[2] or b[1] >= a[2]:
            return False
        return not (a[3] == b[3] and a[3] > 1 and (a[1] - b[1]) % a[3])

    def note(r, write, tok):
        r = span(r)
        h = hist.setdefault(r[0], [])
        if write and r[3] == 1:
            h[:] = [e for e in h if not (r[1] <= e[0][1] and e[0][2] <= r[2])]
        h.append((r, write, tok))

    def wait(q, need):
        for sem in sorted(need):
            val = need[sem]
            if known[q].get(sem, 0) >= val:
                continue
            if any(o != sem and known[q].get(o, 0) < need[o] and snaps.get((o, need[o]), {}).get(sem, 0) >= val for o in need):
                continue
            queues[q].wait_ge(T.sem[sem], val)
        for sem in need:
            known[q][sem] = max(known[q].get(sem, 0), need[sem])
            for s, v in snaps.get((sem, need[sem]), {}).items():
                known[q][s] = max(known[q].get(s, 0), v)

    def deps(reads, writes):
        need = {}
        for rs, w in ((reads, False), (writes, True)):
            for r in rs:
                r = span(r)
                for e, ew, tok in hist.get(r[0], []):
                    if (w or ew) and meet(r, e):
                        need[tok[0]] = max(need.get(tok[0], 0), tok[1])
        return need

    def emit(q, call, reads, writes, sem=None, inc=1):
        wait(q, deps(reads, writes))
        name = sem or own[q]
        call().then_inc(T.sem[name], inc)
        count[name] = count.get(name, 0) + inc
        tok = (name, count[name])
        snaps[tok] = dict(known[q])
        for r in reads:
            note(r, False, tok)
        for r in writes:
            note(r, True, tok)

    def arrive(r, sem, val):
        note(r, True, (sem, val))

    def ready(q, reads):
        wait(q, deps(reads, []))

    return emit, arrive, ready, count


def rank_program(g, core, T, topo):
    rank = T.rank_of(core)
    if rank is None:
        return
    emit, arrive, ready, count = make_tracker(g, T)
    V, S, PE = g.vector, g.scalar, g.tensor

    def R(n, lo, hi, st=1):
        return (n, lo, hi, st)

    def ap(r):
        return T[r[0]][:, r[1]:r[2]] if r[3] == 1 else T[r[0]][:, r[1]:r[2]:r[3]]

    def src(r, off):
        return ap(r) if off is None else ap(r).indirect(ap(off))

    def rd(*rs):
        return [r for r in rs if isinstance(r, tuple)]

    def val(x):
        return ap(x) if isinstance(x, tuple) else x

    def copy(out, in_, off=None):
        emit("v", lambda: V.tensor_copy(ap(out), src(in_, off)), rd(in_, off), [out])

    def ts(out, in_, s1, op0, s2=None, op1=None, off=None):
        if op1 is None:
            emit("v", lambda: V.tensor_scalar(ap(out), src(in_, off), val(s1), None, op0), rd(in_, off, s1), [out])
        else:
            emit("v", lambda: V.tensor_scalar(ap(out), src(in_, off), val(s1), val(s2), op0, op1), rd(in_, off, s1, s2), [out])

    def tt(out, a, b, op, off=None):
        emit("v", lambda: V.tensor_tensor(ap(out), src(a, off), ap(b), op), rd(a, b, off), [out])

    def tr(out, in_):
        emit("v", lambda: V.transpose(ap(out), ap(in_)), [in_], [out])

    def ms(out, c):
        emit("v", lambda: V.memset(ap(out), c), [], [out])

    def qm(q, s, in_):
        emit("v", lambda: V.quantize_mx(ap(q), ap(s), ap(in_)), [in_], [q, s])

    def act(out, in_, off=None, scale=1.0, bias=None):
        if bias is not None:
            emit("s", lambda: S.activation(ap(out), src(in_, off), AF.Identity, bias=ap(bias)), rd(in_, off, bias), [out])
            return
        func = AF.Identity if isinstance(scale, tuple) else AF.Copy
        emit("s", lambda: S.activation(ap(out), src(in_, off), func, scale=val(scale)), rd(in_, off, scale), [out])

    def mm(bank, n, w, ws, x, xs):
        out = R("ps", 512 * bank, 512 * bank + n)
        emit("t", lambda: PE.matmul_mx(ap(out), ap(w), ap(ws), ap(x), ap(xs), True, True), [w, ws, x, xs], [out])
        return out

    def load(q, out, in_ap, sem, code=False):
        eng = {"y": g.sync, "s": g.scalar}[q]
        emit(q, lambda: eng.dma_start(ap(out).bitcast(dt.uint8) if code else ap(out), in_ap), [], [out], sem, 16)

    def iota(out, pattern, base, cm):
        emit("g", lambda: g.iota(ap(out), pattern, base, cm, allow_small_or_imprecise_dtypes=True), [], [out])

    load("s", R("tbi", 0, 22), T.pl[:], "ldp")
    load("y", R("x0", 4 * F, 4 * C), T.x[:, 4 * F:4 * C], "ldx1")
    load("s", R("tbi", 22, 44), T.dl[:], "ldd")
    load("y", R("x0", 0, 4 * F), T.x[:, 0:4 * F], "ldx0")
    load("s", R("tbi", 44, 66), T.kl[:], "ldk")
    load("s", R("ut", 0, 512), T.u[:], "ldu")
    load("y", R("wq", 0, 512), T.wc[:], "ldwc", True)
    load("y", R("wp", 0, 512), T.ws[:], "ldws")
    load("y", R("vt", 0, 512), T.v[:], "ldv")

    ip = R("ci", 0, 1)
    emit("g", lambda: g.iota(ap(ip), [[0, 1]], 0, 1), [], [ip])
    iota(R("rc", 0, 5), [[0, 5]], 1000, 0)
    iota(R("rc", 5, 17), [[0, 4], [22, 3]], 0, 0)
    iota(R("rc", 16, 21), [[0, 5]], 1000, 0)
    iota(R("rc", 21, 33), [[0, 4], [22, 3]], 0, 0)
    iota(R("i2", 0, 22), [[2, 11], [0, 2]], 0, 0)
    iota(R("gam", 0, 24), [[32, 12], [0, 2]], ROT + 176 - 16, 0)
    iota(R("gam", 24, 46), [[32, 11], [0, 2]], ROT + 176, 0)
    iota(R("ones", 0, 512), [[0, 512]], 1, 0)
    for b in range(4):
        e = R("eb", 512 * b, 512 * b + 512)
        emit("g", lambda: g.affine_select(ap(e), ap(R("ones", 0, 512)), [[-1, 512]], AO.is_equal, 0.0, b, 4), [R("ones", 0, 512)], [e])
    ms(R("tbs", 224, 256), 0.0)
    ms(R("tbs", 66, 96), 0.0)
    for n, a in (("ttb", 0), ("ttb", 112), ("tf", 352), ("gl", 0), ("gl", 368), ("wa", 0), ("wa", 368), ("wb", 0), ("wb", 368),
                 ("gb", 0), ("gb", 368), ("n1", 736), ("n2", 736), ("mf", 0), ("mo", 368)):
        act(R(n, a, a + 16), R("tbs", 224, 240))
    act(R("sm", 384, 400), R("tbs", 224, 240))
    act(R("sm", 400, 432), R("tbs", 224, 256))
    def cf(i):
        return R("cf", i, i + 1)

    def ci(i):
        return R("ci", i, i + 1)
    ts(ci(1), ip, 15, AO.bitwise_and)
    ts(ci(2), ip, 4, AO.arith_shift_right, 1, AO.bitwise_and)
    ts(ci(3), ip, 31, AO.bitwise_and)
    tr(R("lc", 0, 32), R("rc", 0, 32))
    copy(R("cf", 0, 3), R("ci", 1, 4))
    tt(ci(4), ci(1), ci(2), AO.add)
    q_, par, i32, l32, odd = cf(0), cf(1), cf(2), R("lc", 0, 1), cf(3)
    ts(cf(4), par, 97.0, AO.mult)
    ts(cf(5), par, -127.0, AO.mult, 128.0, AO.add)
    ts(ci(5), ci(4), 1, AO.bitwise_and)
    tt(cf(6), cf(4), l32, AO.add)
    tt(cf(7), cf(5), l32, AO.add)
    copy(odd, ci(5))
    ts(cf(6), cf(6), 224.0, AO.min)
    ts(cf(7), cf(7), 224.0, AO.min)
    ts(R("offi", 0, 22, 2), R("i2", 0, 22, 2), cf(6), AO.add)
    ts(R("offi", 1, 22, 2), R("i2", 1, 22, 2), cf(7), AO.add)
    RM, THR, WT, NB = cf(8), cf(9), cf(19), cf(20)

    ts(R("tbs", 0, 66), R("tbi", 0, 66), float(-MID), AO.add)
    copy(R("opi", 0, 22), R("tbi", 0, 22))
    tr(R("ttb", 16, 112), R("tbs", 0, 96))
    tr(R("tbs", 96, 224), R("ttb", 0, 128))
    copy(R("tf", 0, 352), R("tbs", 0, 256), R("offi", 0, 22))
    tr(R("wa", 16, 368), R("tf", 0, 352))
    GAM = R("gam", 0, 46)

    def sm(i):
        return R("sm", 48 * i, 48 * i + 46)

    PM, PP, PK, PK1, PO, PD = R("pk", 0, 2), R("pk", 2, 4), R("pk", 4, 6), R("pk", 4, 5), R("pk", 6, 7), R("pk", 8, 10)

    def prelinks(off):
        act(R("gl", 16, 368), R("wa", 16, 368), off)

    def prelinks2():
        tr(R("glt", 0, 384), R("gl", 0, 384))
        tr(R("glt", 384, 736), R("gl", 16, 368))

    def prelinks3():
        for o, pick, a in (("td", PD, 1088), ("tp", PP, 1440)):
            ts(R(o, 0, 32), R("glt", 0, 736), float(MID), AO.add, off=pick)
            act(R("wa", a, a + C), R("wa", 16, 368), R(o, 0, 22))

    def prelinks4():
        act(R("wr", 704, 1056), R("wa", 384, 736), R("td", 0, 22))
        act(R("wr", 1056, 1408), R("wa", 384, 736), R("tp", 0, 22))

    prelinks(R("opi", 0, 22))
    act(R("wa", 736, 1088), R("wa", 16, 368))
    ts(cf(10), odd, -23.0, AO.mult, 24.0, AO.add)
    ts(THR, q_, 3.5, AO.is_ge, 1e28, AO.mult)
    ts(cf(17), q_, 0.0, AO.is_equal, 352.0, AO.mult)
    ts(cf(18), q_, 2.0, AO.is_equal, 1696.0, AO.mult)
    tt(cf(11), cf(10), q_, AO.add)
    ts(WT, cf(17), cf(18), AO.add, 352.0, AO.add)
    ts(cf(12), cf(11), 16.0, AO.add, 45.0, AO.min)
    ts(PP, R("cf", 11, 13), 16.0, AO.mult, 5.0, AO.add)
    ts(PD, R("cf", 11, 13), 16.0, AO.mult, 6.0, AO.add)
    copy(PM, R("cf", 11, 13))
    rest = [
        lambda: ts(GAM, GAM, i32, AO.add),
        lambda: ts(cf(21), q_, 2.0, AO.is_equal, -1024.0, AO.mult),
        lambda: ts(cf(22), q_, 3.0, AO.is_equal, -176.0, AO.mult),
        lambda: tt(NB, cf(21), cf(22), AO.add),
        lambda: ts(RM, l32, 500.0, AO.is_lt),
        lambda: ts(PK, R("cf", 11, 13), 16.0, AO.mult, 7.0, AO.add),
        lambda: ts(cf(14), odd, 23.0, AO.mult, 12.0, AO.add),
        lambda: ms(cf(23), float(MID)),
        lambda: tt(cf(15), cf(14), q_, AO.add),
        lambda: ts(cf(16), cf(15), 45.0, AO.min, 16.0, AO.mult),
        lambda: ts(PO, cf(16), 7.0, AO.add),
    ]

    def fill(n):
        for i in range(n):
            if rest:
                rest.pop(0)()

    def state_half(r, h):
        lo, hi = (0, F) if h == 0 else (F, C)
        qm(R("qx", lo, hi), R("sx", lo, hi), R("x%d" % r, 4 * lo, 4 * hi))

    def signs_mm(h):
        lo, hi = (0, F) if h == 0 else (F, C)
        mm(5 - h, F, R("qu", 0, 128), R("su", 0, 128), R("qx", lo, hi), R("sx", lo, hi))

    def signs_ts(h):
        lo, hi = (0, F) if h == 0 else (F, C)
        ts(R("bt", lo, hi), R("ps", 512 * (5 - h), 512 * (5 - h) + F), THR, AO.is_gt, WT, AO.mult)

    def planes(r, h):
        lo, hi = (0, F) if h == 0 else (F, C)
        for t in range(4):
            act(R("xp", C * t + lo, C * t + hi), R("x%d" % r, 4 * lo + t, 4 * hi, 4), scale=0.5)

    prelinks2()
    prelinks3()
    state_half(0, 1)
    qm(R("qu", 0, 128), R("su", 0, 128), R("ut", 0, 512))
    state_half(0, 0)
    tr(R("wa", 384, 736), R("tf", 1, 353))
    signs_mm(1)
    signs_mm(0)
    signs_ts(1)
    signs_ts(0)

    ALL = R("wa", 384, 1792)
    ALLB = R("wb", 16, 1088)

    def turn(dst, srcb, a, b):
        tr(R(dst, 384 + a, 384 + b), R(srcb, 16 + a, 16 + b))
        e = 384 if b == C else b
        tr(R(dst, a, e), R(srcb, a, e))

    dst = T.cores[0]
    offp = R("opi", 0, 22)
    for r in range(3):
        s = STEP[r]
        source, target = T.cores[(rank - s) % 8], T.cores[(rank + s) % 8]
        last = r == 2
        n_all = len(topo.engines(core, target))
        PIN = R("pin%d" % r, 0, 12)
        arrive(PIN, "ap%d" % r, len(topo.engines(source, core)))
        arrive(R("kin%d" % r, 0, 22), "ak%d" % r, n_all)
        arrive(R("qin%d" % r, 0, F), "ac%d" % r, n_all)
        arrive(R("sin%d" % r, 0, F), "as%d" % r, n_all)
        X, XN = "x%d" % r, "x%d" % (r + 1)

        k = 10
        a = 16 * k
        BT = R("bt", 0, C)
        copy(R("gb", 16, 16 + a), BT, R(offp[0], 0, k))
        act(R("gb", 16 + a, 368), BT, R(offp[0], k, 22))
        turn("gt", "gb", 0, a)
        turn("gt", "gb", a, C)
        A0, A1 = R("gt", 0, 736, 16), R("gt", 1, 736, 16)
        tt(sm(3), A0, A1, AO.add)
        fill(1)
        tt(sm(8), sm(3), GAM, AO.add)
        fill(1)
        ts(R("o1", 0, 32), R("sm", 48 * 8, 48 * 9), float(-ROT - 176), AO.add, off=PM)
        fill(1)
        tt(R("wb", 16, 368), ALL, BT, AO.add, off=R("o1", 0, 22))
        if r == 0:
            act(R("wb", 736, 1088), R("wa", 736, 1088))
            planes(0, 1)
        else:
            act(R("wb", 384, 736), R("wr", 0, 1408), R("o1", 0, 22))
        planes(r, 0)
        fill(1)
        turn("n1", "wb", 0, C)
        fill(1)
        ts(R("op1", 0, 32), R("n1", 0, 736), float(MID), AO.add, off=PP)
        fill(1)

        k = 8 if r == 0 else 10
        a = 16 * k
        CB = R("wb", 16, 368)
        act(R("gb", 16 + a, 368), CB, R("op1", k, 22), bias=NB)
        ts(R("gb", 16, 16 + a), CB, NB, AO.add, off=R("op1", 0, k))
        turn("gt", "gb", 0, a)
        if r == 0:
            tr(R("wb", 384, 736), R("n1", 385, 737))
        turn("gt", "gb", a, C)
        A2, A3, GP, GD = R("gt", 2, 736, 16), R("gt", 3, 736, 16), R("gt", 5, 736, 16), R("gt", 6, 736, 16)
        tt(sm(1), GP, A3, AO.add)
        tt(sm(2), GD, A3, AO.subtract)
        tt(sm(3), GAM, A3, AO.add)
        tt(sm(4), sm(1), sm(2), AO.max)
        tt(sm(5), sm(3), A2, AO.subtract)
        tt(sm(6), sm(4), A2, AO.add)
        fill(1)
        tt(sm(8), sm(6), sm(5), AO.max)
        fill(1)
        ts(R("o2", 0, 32), R("sm", 48 * 8, 48 * 9), -1024.0, AO.add, off=PM)
        fill(1)
        k = 10
        a = 16 * k
        act(R("wa", 16 + a, 368), ALLB, R("o2", k, 22), scale=RM)
        ts(R("wa", 16, 16 + a), ALLB, RM, AO.mult, off=R("o2", 0, k))
        turn("n2", "wa", 0, a)
        turn("n2", "wa", a, C)
        fill(1)
        OP = "opn%d" % r
        N2 = R("n2", 0, 736)
        ts(R(OP, 0, 32), N2, float(MID), AO.add, off=PP)
        KS = R("ks%d" % r, 0, 22)
        copy(KS, R("n2", 384 + 7, 736, 16))
        ts(R("ok", 0, 32), N2, float(MID), AO.add, off=PK)
        offp = R(OP, 0, 22)

        for d, sr, ds, sem in ((source, R(OP, 0, 12), PIN, "ap%d" % r), (target, KS, R("kin%d" % r, 0, 22), "ak%d" % r)):
            ready("g", [sr])
            rid, pid = topo.addr(d, core)
            g.remote_dma(ap(ds), ap(sr), T.sem[sem], T.sem["sent"], pid, rid, topo.mask(core, d))
            count["sent"] = count.get("sent", 0) + len(topo.engines(core, d))

        if not last:
            tr(R("wa", 384, 736), R("n2", 385, 737))
        fill(20)
        for c, (k0, k1) in enumerate(((0, 12), (12, 22))):
            lo, hi = 16 * k0, 16 * k1
            for t in range(4):
                win = R("xp", C * t, C * t + C)
                zp = R("zp", C * t + lo, C * t + hi)
                act(zp, win, R(OP, k0, k1))
                tt(R("zt", 4 * lo + t, 4 * hi, 4), win, zp, AO.add, off=R("ok", k0, k1))
            qm(R("qz", lo, hi), R("sz", lo, hi), R("zt", 4 * lo, 4 * hi))
            for b in range(4):
                mm(4 * c + b, hi - lo, R("wq", 128 * b, 128 * b + 128), R("wp", 128 * b, 128 * b + 128), R("qz", lo, hi), R("sz", lo, hi))

        def evict(c, b):
            lo, w = (0, 192) if c == 0 else (192, 160)
            bank = 512 * (4 * c + b)
            act(R("hp", C * b + lo, C * b + lo + w), R("ps", bank, bank + w), scale=0.03125)

        for b in range(3):
            evict(0, b)
        act(R("mf", 16, 208), R("wa", 16, 368), R("pin%d" % r, 0, 12))
        evict(0, 3)
        if r == 0:
            for b in range(4):
                qm(R("qe", 128 * b, 128 * b + 128), R("se", 128 * b, 128 * b + 128), R("eb", 512 * b, 512 * b + 512))
        if r == 1:
            qm(R("qv", 0, 128), R("sv", 0, 128), R("vt", 0, 512))
        turn("gt", "mf", 0, 192)
        ts(R("om", 0, 16), R("gt", 0, 736), float(MID), AO.add, off=PK1)
        for b in range(4):
            evict(1, b)
            ft = R("ft", b, 4 * F, 4)
            hw = R("hp", C * b, C * b + C)
            if b < 3:
                copy(ft, hw, R("om", 0, 11))
            else:
                act(ft, hw, R("om", 0, 11))
        qm(R("qf%d" % r, 0, F), R("sf%d" % r, 0, F), R("ft", 0, 4 * F))

        QF, SF = R("qf%d" % r, 0, F), R("sf%d" % r, 0, F)
        ready("g", [QF, SF])
        rid, pid = topo.addr(target, core)
        m = topo.mask(core, target)
        g.remote_dma(ap(R("qin%d" % r, 0, F)).bitcast(dt.uint8), ap(QF).bitcast(dt.uint8), T.sem["ac%d" % r], T.sem["sent"], pid, rid, m)
        g.remote_dma(ap(R("sin%d" % r, 0, F)), ap(SF), T.sem["as%d" % r], T.sem["sent"], pid, rid, m)
        count["sent"] += 2 * n_all

        if not last:
            prelinks(offp)
        copy(R("n1", 384 + 7, 736, 16), R("kin%d" % r, 0, 22))
        tr(R("kr", 0, C), R("n1", 384, 736))
        act(R("mo", 176, 368), R("kr", 0, C), R(OP, 10, 22))
        if not last:
            prelinks2()
            prelinks3()
        tr(R("gt", 384 + 160, 736), R("mo", 176, 368))
        tr(R("gt", 192, 384), R("mo", 192, 384))
        ts(R("oo", 0, 16), R("gt", 0, 736), float(MID), AO.add, off=PO)
        for t in range(4):
            tt(R(XN, 4 * F + t, 4 * C, 4), R("hp", C * t, C * t + C), R(X, 4 * F + t, 4 * C, 4), AO.add, off=R("oo", 0, 11))
        state_half(r + 1, 1)
        if not last:
            planes(r + 1, 1)
            prelinks4()
            signs_mm(1)
            tr(R("wr", 0, 352), R("n2", 386, 738))
            if r == 0:
                tr(R("wr", 352, 704), R("tf", 1, 353))
        else:
            store(g, T, emit, ap, R, mm, act, ts, 1)
            lkt = R("lkt", 0, C)
            act(lkt, R("wa", 16, 368), bias=cf(23))
            for gr in range(8):
                emit("y", lambda: g.sync.dma_start(T.lk[gr:gr + 1, :], T.lkt[16 * gr + 5:16 * gr + 8, :]), [lkt], [], "sty", 16)

        for b in range(4):
            out = mm(b, F, R("qe", 128 * b, 128 * b + 128), R("se", 128 * b, 128 * b + 128), R("qin%d" % r, 0, F), R("sin%d" % r, 0, F))
            tt(R(XN, b, 4 * F, 4), out, R(X, b, 4 * F, 4), AO.add)
        state_half(r + 1, 0)
        if not last:
            signs_ts(1)
            signs_mm(0)
            signs_ts(0)
        else:
            store(g, T, emit, ap, R, mm, act, ts, 0)

    for n in ("cv", "cs", "ct", "cg", "sent", "sty", "sta"):
        if count.get(n):
            g.wait_ge(T.sem[n], count[n])


def store(g, T, emit, ap, R, mm, act, ts, h):
    lo, hi = (0, F) if h == 0 else (F, C)
    Q, P, Y = R("qx", lo, hi), R("sx", lo, hi), R("yt", lo, hi)
    out = mm(5 - h, F, R("qv", 0, 128), R("sv", 0, 128), Q, P)
    emit("y", lambda: g.sync.dma_start(T.oc[:, 4 * lo:4 * hi], ap(Q).bitcast(dt.uint8)), [Q], [], "sty", 16)
    for k in range(4):
        q, e, sem = ("s", g.scalar, "sta") if k % 2 else ("y", g.sync, "sty")
        emit(q, lambda: e.dma_start(T.osc[4 * k:4 * k + 4, lo:hi], T.sx[32 * k:32 * k + 4, lo:hi]), [P], [], sem, 16)
    if h:
        act(Y, out)
    else:
        ts(Y, out, 1.0, AO.mult)
    emit("y", lambda: g.sync.dma_start(T.y[:, lo:hi], ap(Y)), [Y], [], "sty", 16)
